import numpy as np
import ml_dtypes


def mxq(x, axis, fmt="e4m3"):
    dtype, down = {"e4m3": (ml_dtypes.float8_e4m3fn, 7), "e5m2": (ml_dtypes.float8_e5m2, 14)}[fmt]
    v = np.moveaxis(np.asarray(x, np.float32).astype(ml_dtypes.bfloat16).astype(np.float64), axis, -1)
    blocks = v.reshape(v.shape[:-1] + (-1, 32))
    amax = np.abs(blocks).max(-1, keepdims=True)
    byte = np.maximum(np.where(amax > 0, np.frexp(amax)[1] - 1 + 127, 0) - down, 1)
    scale = np.exp2(byte - 127.0)
    codes = (blocks / scale).astype(np.float32).astype(dtype).astype(np.float64)
    return np.moveaxis((codes * scale).reshape(v.shape), -1, axis)


WIDE = False


def mx_kscale(k):
    if not WIDE:
        return np.ones(k)
    levels = np.array([10, -10, 5, -5, 0])
    if k % 512:
        return np.exp2(np.random.permutation(np.resize(levels, k // 32))).repeat(32)
    a = np.empty((k // 512, 16))
    for p in range(k // 512):
        a[p, :8] = np.random.permutation(np.resize(levels, 8))
        for g in range(8):
            far = levels[np.abs(levels - a[p, g]) >= 10]
            a[p, g + 8] = far[np.random.randint(len(far))]
    return np.exp2(a.ravel()).repeat(32)


def f64(x):
    return np.asarray(x).astype(np.float64)


def striped(idx):
    return np.tile(idx.reshape(-1, 16).T, (8, 1)).astype(np.uint16)


def unstriped(offs):
    return offs[:16].T.reshape(-1).astype(np.int64)


E2M1 = np.array([0.0, 0.5, 1.0, 1.5, 2.0, 3.0, 4.0, 6.0, -0.0, -0.5, -1.0, -1.5, -2.0, -3.0, -4.0, -6.0])


def pack_weight(w, fmt):
    k, n = w.shape
    w = f64(np.asarray(w, np.float32).astype(ml_dtypes.bfloat16)).reshape(k // 32, 32, n)
    amax = np.abs(w).max(1)
    if fmt == "e4m3":
        byte = np.frexp(amax)[1] - 1 + 127 - 7
    else:
        mant, ex = np.frexp(amax / 6.0)
        byte = np.where(mant > 0.5, ex, ex - 1) + 127
    byte = np.clip(np.where(amax > 0, byte, 1), 1, 254)
    scaled = (w * np.exp2(127.0 - byte)[:, None, :]).reshape(k, n).astype(np.float32)
    by_word = np.ascontiguousarray(scaled.reshape(k // 512, 128, 4, n).transpose(0, 1, 3, 2))
    if fmt == "e4m3":
        words = by_word.astype(ml_dtypes.float8_e4m3fn).view(np.uint8)
    else:
        c = by_word.astype(ml_dtypes.float4_e2m1fn).view(np.uint8) & 0xF
        words = (c[..., 0::2] | (c[..., 1::2] << 4)).reshape(k // 512, 128, 2 * n)
    return np.ascontiguousarray(words), np.ascontiguousarray(byte.astype(np.uint8).reshape(k // 512, 16, n))


def unpack_weight(words, scales, fmt):
    g, _, n = scales.shape
    words = np.ascontiguousarray(words).reshape(g, 128, n, -1)
    if fmt == "e4m3":
        vals = words.view(ml_dtypes.float8_e4m3fn).astype(np.float64)
    else:
        nib = np.empty((g, 128, n, 4), np.uint8)
        nib[..., 0::2] = words & 0xF
        nib[..., 1::2] = words >> 4
        vals = E2M1[nib]
    vals = vals * np.repeat(np.exp2(scales.astype(np.float64) - 127.0), 8, axis=1)[..., None]
    return vals.transpose(0, 1, 3, 2).reshape(g * 512, n)


def silu(v):
    return v / (1.0 + np.exp(-np.maximum(v, -700.0)))


K, M, T, S = 1024, 1024, 4096, 2048


def setup_inputs():
    n = np.random.standard_normal
    s = mx_kscale(K)[:, None]
    u = mx_kscale(512)[:, None]
    v = pack_weight(n((K, T)) * s, "e4m3")
    p_w4 = pack_weight(n((K, M)) / np.sqrt(K) / s, "e2m1")
    return {
        "tab_words": v[0],
        "tab_scales": v[1],
        "w4_words": p_w4[0],
        "w4_scales": p_w4[1],
        "down": (n((K, 512)) / np.sqrt(K) / s * u.T).astype(np.float32),
        "up": (0.5 * n((512, M)) / np.sqrt(512) / u).astype(np.float32),
        "rT": n((M, T)).astype(np.float32),
        "b": (0.3 * n(1024)).astype(np.float32),
        "offs": striped(np.random.permutation(T)[:S]),
    }


def reference(tab_words, tab_scales, w4_words, w4_scales, down, up, rT, b, offs):
    tab_ = unpack_weight(tab_words, tab_scales, "e4m3")[:, unstriped(offs)]
    w4_ = unpack_weight(w4_words, w4_scales, "e2m1")
    down_ = mxq(f64(down), 0, "e4m3")
    up_ = mxq(f64(up), 0, "e4m3")
    h_ = mxq(down_.T @ tab_, 0, "e4m3")
    y = w4_.T @ tab_ + up_.T @ h_
    return (silu(y + f64(b)[:, None])) + f64(rT)[:, unstriped(offs)]

@@ -1,0 +1,207 @@
+from contextlib import ExitStack
+
+import concourse.mybir as mybir
+from concourse.masks import make_identity
+
+K, M, T, S, R = 1024, 1024, 4096, 2048, 512
+FLOPS = 2 * S * (K * R + K * M + R * M)
+
+F32 = mybir.dt.float32
+BF16 = mybir.dt.bfloat16
+I32 = mybir.dt.int32
+U32 = mybir.dt.uint32
+U16 = mybir.dt.uint16
+U8 = mybir.dt.uint8
+FP8X4 = mybir.dt.float8_e4m3fn_x4
+FP4X4 = mybir.dt.float4_e2m1fn_x4
+ACT = mybir.ActivationFunctionType
+ADD = mybir.AluOpType.add
+
+P = 128
+PACK = 4
+PASSES = K // (P * PACK)
+CHUNK = 512
+CHUNKS = S // CHUNK
+ROW_TILES = M // P
+PIECE = 1024
+LIST_ROWS = 16
+BIG_BUFS = 6
+OUT_BUFS = 6
+
+
+def tile_list_tabres_silu_kernel(
+    tc, tab_words, tab_scales, w4_words, w4_scales, down, up, rT, b, offs, out
+):
+    nc = tc.nc
+    with ExitStack() as ctx:
+        keep = ctx.enter_context(tc.tile_pool(name="keep", bufs=1))
+        big = ctx.enter_context(tc.tile_pool(name="big", bufs=BIG_BUFS))
+        reused = ctx.enter_context(tc.tile_pool(name="reused", bufs=1))
+        stage = ctx.enter_context(tc.tile_pool(name="stage", bufs=4))
+        acts = ctx.enter_context(tc.tile_pool(name="acts", bufs=4))
+        outs = ctx.enter_context(tc.tile_pool(name="outs", bufs=OUT_BUFS))
+        psum_h = ctx.enter_context(tc.psum_pool(name="psum_h", bufs=4))
+        psum_y = ctx.enter_context(tc.psum_pool(name="psum_y", bufs=4))
+
+        offsets = keep.tile([P, S // LIST_ROWS], U16, name="offsets")
+        nc.sync.dma_start(offsets[:], offs)
+
+        def picks(first, count):
+            return offsets[:, first // LIST_ROWS : (first + count) // LIST_ROWS]
+
+        table = []
+        table.append(big.tile([P, T], U32, name="table0", tag="big", align_bytes=64))
+        nc.sync.dma_start(table[0][:].bitcast(I32), tab_words[0].rearrange("p t i -> p (t i)").bitcast(I32))
+        down_raw = big.tile([P, PASSES, PACK, R], F32, name="down_raw", tag="big", align_bytes=64)
+        nc.sync.dma_start(down_raw[:], down.rearrange("(a p i) r -> p a i r", a=PASSES, i=PACK))
+        table.append(big.tile([P, T], U32, name="table1", tag="big", align_bytes=64))
+        nc.sync.dma_start(table[1][:].bitcast(I32), tab_words[1].rearrange("p t i -> p (t i)").bitcast(I32))
+        up_raw = big.tile([P, PACK, M], F32, name="up_raw", tag="big", align_bytes=64)
+        nc.sync.dma_start(up_raw[:], up.rearrange("(p i) n -> p i n", i=PACK))
+        w4_codes = keep.tile([P, PASSES, 2 * M], U8, name="w4_codes", align_bytes=64)
+        nc.sync.dma_start(w4_codes[:].bitcast(I32), w4_words.rearrange("a p n -> p a n").bitcast(I32))
+        residual = []
+        for n in range(ROW_TILES):
+            rows = big.tile([P, T], F32, name=f"residual{n}", tag="big", align_bytes=64)
+            nc.sync.dma_start(rows[:], rT[n * P : (n + 1) * P, :])
+            residual.append(rows)
+
+        tab_plane = reused.tile([P, T], U8, name="tab_plane", align_bytes=64, offset=7168)
+        w4_plane = keep.tile([P, PASSES, M], U8, name="w4_plane", align_bytes=64)
+        bias_rows = keep.tile([P, P], F32, name="bias_rows")
+        moved_plane = keep.tile([P, S], U8, name="moved_plane", align_bytes=64)
+        nc.vector.memset(tab_plane[:].bitcast(I32), 0)
+        nc.vector.memset(w4_plane[:].bitcast(I32), 0)
+        nc.vector.memset(bias_rows[:], 0.0)
+        nc.vector.memset(moved_plane[:].bitcast(I32), 0)
+        for q in range(4):
+            nc.gpsimd.dma_start(
+                tab_plane[32 * q : 32 * q + 4 * PASSES, :].bitcast(I32),
+                tab_scales[:, 4 * q : 4 * q + 4, :].bitcast(I32),
+            )
+        for q in range(4):
+            nc.gpsimd.dma_start(
+                w4_plane[32 * q : 32 * q + 4, :, :].bitcast(I32),
+                w4_scales[:, 4 * q : 4 * q + 4, :].rearrange("a r n -> r a n").bitcast(I32),
+            )
+        nc.gpsimd.dma_start(bias_rows[0:ROW_TILES, :], b.rearrange("(n p) -> n p", p=P))
+        identity = keep.tile([P, P], F32, name="identity")
+        make_identity(nc, identity[:])
+        bias_bank = psum_h.tile([P, PACK, P], F32, name="bias_bank", tag="h_bank")
+        nc.tensor.transpose(bias_bank[:, 0, :], bias_rows[:], identity[:])
+        bias = keep.tile([P, ROW_TILES], F32, name="bias")
+        nc.scalar.copy(bias[:], bias_bank[:, 0, 0:ROW_TILES])
+
+        words0 = keep.tile([P, S], U32, name="words0", align_bytes=64)
+        nc.vector.tensor_copy(words0[:], table[0][:].indirect(offsets[:]))
+        picked_plane = keep.tile([P, S], U8, name="picked_plane", align_bytes=64)
+        nc.vector.tensor_copy(picked_plane[:], tab_plane[:].indirect(offsets[:]))
+        for q in range(4):
+            nc.gpsimd.dma_start(
+                moved_plane[32 * q : 32 * q + 4, :].bitcast(I32),
+                picked_plane[32 * q + 4 : 32 * q + 8, :].bitcast(I32),
+            )
+
+        down_codes, down_plane = [], []
+        for a in range(PASSES):
+            grouped = stage.tile([P, PACK * R], BF16, name=f"down_bf16_{a}", tag="grouped", align_bytes=64)
+            nc.scalar.copy(
+                grouped[:].rearrange("p (t m i) -> p m t i", t=PACK, i=PACK),
+                down_raw[:, a].rearrange("p i (m t) -> p m t i", t=PACK),
+            )
+            codes = keep.tile([P, R], U32, name=f"down_codes{a}", align_bytes=64)
+            plane = reused.tile([P, R], U8, name=f"down_plane{a}", align_bytes=64, offset=8192 + a * R)
+            nc.vector.quantize_mx(out=codes[:].bitcast(FP8X4), scales=plane[:], in_=grouped[:])
+            down_codes.append(codes)
+            down_plane.append(plane)
+
+        words1 = reused.tile([P, S], U32, name="words1", align_bytes=64, offset=0)
+        for c in range(CHUNKS):
+            nc.vector.tensor_copy(
+                words1[:, c * CHUNK : (c + 1) * CHUNK], table[1][:].indirect(picks(c * CHUNK, CHUNK))
+            )
+        words = [words0, words1]
+
+        def moving_words(a, first, count):
+            return words[a][:, first : first + count].bitcast(FP8X4)
+
+        up_codes, up_plane = [], []
+        up_grouped = reused.tile([P, PACK * M], BF16, name="up_grouped", align_bytes=64, offset=8192 + PASSES * R)
+        for half in range(M // CHUNK):
+            grouped = up_grouped[:, half * PACK * CHUNK : (half + 1) * PACK * CHUNK]
+            nc.vector.tensor_copy(
+                grouped.rearrange("p (c e i) -> p c i e", e=4, i=PACK),
+                up_raw[:, :, half * CHUNK : (half + 1) * CHUNK].rearrange("p i (c e) -> p c i e", e=4),
+            )
+            codes = keep.tile([P, CHUNK], U32, name=f"up_codes{half}", align_bytes=64)
+            plane = keep.tile([P, CHUNK], U8, name=f"up_plane{half}", align_bytes=64)
+            nc.vector.quantize_mx(out=codes[:].bitcast(FP8X4), scales=plane[:], in_=grouped)
+            up_codes.append(codes)
+            up_plane.append(plane)
+
+        h_codes, h_plane = [], []
+        for c in range(CHUNKS):
+            grouped = stage.tile([P, PACK * CHUNK], BF16, name=f"h_bf16_{c}", tag="grouped", align_bytes=64)
+            for block in range(CHUNK // P):
+                first = c * CHUNK + block * P
+                bank = psum_h.tile([P, PACK, P], F32, name=f"h_bank{c}_{block}", tag="h_bank")
+                for t in range(PACK):
+                    for a in range(PASSES):
+                        nc.tensor.matmul_mx(
+                            out=bank[:, t, :],
+                            lhsT=down_codes[a][:, t * P : (t + 1) * P].bitcast(FP8X4),
+                            lhsT_scale=down_plane[a][:, t * P : (t + 1) * P],
+                            rhs=moving_words(a, first, P),
+                            rhs_scale=picked_plane[4 * a :, first : first + P],
+                            start=(a == 0),
+                            stop=(a == PASSES - 1),
+                        )
+                nc.scalar.copy(
+                    grouped[:, block * P * PACK : (block + 1) * P * PACK].rearrange("p (j t) -> p j t", t=PACK),
+                    bank[:].rearrange("p t j -> p j t"),
+                )
+            codes = keep.tile([P, CHUNK], U32, name=f"h_codes{c}", align_bytes=64)
+            plane = keep.tile([P, CHUNK], U8, name=f"h_plane{c}", align_bytes=64)
+            nc.vector.quantize_mx(out=codes[:].bitcast(FP8X4), scales=plane[:], in_=grouped[:])
+            h_codes.append(codes)
+            h_plane.append(plane)
+
+        word_planes = [picked_plane, moved_plane]
+        for n in range(ROW_TILES):
+            half, within = divmod(n * P, CHUNK)
+            result = outs.tile([P, S], F32, name=f"result{n}", tag="result")
+            for piece in range(S // PIECE):
+                activated = acts.tile([P, PIECE], F32, name=f"silu{n}_{piece}", tag="silu")
+                for cc in range(PIECE // CHUNK):
+                    c = piece * (PIECE // CHUNK) + cc
+                    cols = slice(c * CHUNK, (c + 1) * CHUNK)
+                    bank = psum_y.tile([P, CHUNK], F32, name=f"y_bank{n}_{c}", tag="y_bank")
+                    for a in range(PASSES):
+                        nc.tensor.matmul_mx(
+                            out=bank[:],
+                            lhsT=w4_codes[:, a, 2 * n * P : 2 * (n + 1) * P].bitcast(FP4X4),
+                            lhsT_scale=w4_plane[:, a, n * P : (n + 1) * P],
+                            rhs=moving_words(a, c * CHUNK, CHUNK),
+                            rhs_scale=word_planes[a][:, cols],
+                            start=(a == 0),
+                            stop=False,
+                        )
+                    nc.tensor.matmul_mx(
+                        out=bank[:],
+                        lhsT=up_codes[half][:, within : within + P].bitcast(FP8X4),
+                        lhsT_scale=up_plane[half][:, within : within + P],
+                        rhs=h_codes[c][:].bitcast(FP8X4),
+                        rhs_scale=h_plane[c][:],
+                        start=False,
+                        stop=True,
+                    )
+                    nc.scalar.activation(
+                        activated[:, cc * CHUNK : (cc + 1) * CHUNK], bank[:], ACT.Silu, bias=bias[:, n : n + 1]
+                    )
+                nc.vector.tensor_tensor(
+                    result[:, piece * PIECE : (piece + 1) * PIECE],
+                    residual[n][:].indirect(picks(piece * PIECE, PIECE)),
+                    activated[:],
+                    ADD,
+                )
+            nc.sync.dma_start(out[n * P : (n + 1) * P, :], result[:])

@@ -25,7 +25,7 @@ CHUNKS = S // CHUNK
 ROW_TILES = M // P
 PIECE = 1024
 LIST_ROWS = 16
-BIG_BUFS = 6
+SLOT = 4 * T
 OUT_BUFS = 6
 
 
@@ -35,9 +35,8 @@ def tile_list_tabres_silu_kernel(
     nc = tc.nc
     with ExitStack() as ctx:
         keep = ctx.enter_context(tc.tile_pool(name="keep", bufs=1))
-        big = ctx.enter_context(tc.tile_pool(name="big", bufs=BIG_BUFS))
-        reused = ctx.enter_context(tc.tile_pool(name="reused", bufs=1))
-        stage = ctx.enter_context(tc.tile_pool(name="stage", bufs=4))
+        slots = ctx.enter_context(tc.tile_pool(name="slots", bufs=1))
+        stage = ctx.enter_context(tc.tile_pool(name="stage", bufs=3))
         acts = ctx.enter_context(tc.tile_pool(name="acts", bufs=4))
         outs = ctx.enter_context(tc.tile_pool(name="outs", bufs=OUT_BUFS))
         psum_h = ctx.enter_context(tc.psum_pool(name="psum_h", bufs=4))
@@ -49,42 +48,62 @@ def tile_list_tabres_silu_kernel(
         def picks(first, count):
             return offsets[:, first // LIST_ROWS : (first + count) // LIST_ROWS]
 
-        table = []
-        table.append(big.tile([P, T], U32, name="table0", tag="big", align_bytes=64))
-        nc.sync.dma_start(table[0][:].bitcast(I32), tab_words[0].rearrange("p t i -> p (t i)").bitcast(I32))
-        down_raw = big.tile([P, PASSES, PACK, R], F32, name="down_raw", tag="big", align_bytes=64)
-        nc.sync.dma_start(down_raw[:], down.rearrange("(a p i) r -> p a i r", a=PASSES, i=PACK))
-        table.append(big.tile([P, T], U32, name="table1", tag="big", align_bytes=64))
-        nc.sync.dma_start(table[1][:].bitcast(I32), tab_words[1].rearrange("p t i -> p (t i)").bitcast(I32))
-        up_raw = big.tile([P, PACK, M], F32, name="up_raw", tag="big", align_bytes=64)
-        nc.sync.dma_start(up_raw[:], up.rearrange("(p i) n -> p i n", i=PACK))
-        w4_codes = keep.tile([P, PASSES, 2 * M], U8, name="w4_codes", align_bytes=64)
-        nc.sync.dma_start(w4_codes[:].bitcast(I32), w4_words.rearrange("a p n -> p a n").bitcast(I32))
-        residual = []
-        for n in range(ROW_TILES):
-            rows = big.tile([P, T], F32, name=f"residual{n}", tag="big", align_bytes=64)
-            nc.sync.dma_start(rows[:], rT[n * P : (n + 1) * P, :])
-            residual.append(rows)
+        slot_a, slot_b, slot_c, slot_e = 0, SLOT, 2 * SLOT, 3 * SLOT
+        w4_at = 4 * SLOT
+        w4_plane_at = w4_at + 4096
+        slot_d = w4_plane_at + 2048
+        window_at = w4_plane_at - 1024
+        residual_slots = [slot_a, slot_b, slot_c, slot_d, slot_e]
 
-        tab_plane = reused.tile([P, T], U8, name="tab_plane", align_bytes=64, offset=7168)
-        w4_plane = keep.tile([P, PASSES, M], U8, name="w4_plane", align_bytes=64)
+        tab_plane = slots.tile([P, T], U8, name="tab_plane", align_bytes=64, offset=window_at)
+        nc.sync.dma_start(tab_plane[0:32, :].bitcast(I32), tab_scales.rearrange("a q t -> q a t").bitcast(I32))
+        table0 = slots.tile([P, T], U32, name="table0", align_bytes=64, offset=slot_a)
+        nc.sync.dma_start(table0[:].bitcast(I32), tab_words[0].rearrange("p t i -> p (t i)").bitcast(I32))
+        down_raw = []
+        for a in range(PASSES):
+            raw = slots.tile([P, PACK, R], F32, name=f"down_raw{a}", align_bytes=64, offset=slot_b + a * SLOT // 2)
+            nc.sync.dma_start(raw[:], down[a * P * PACK : (a + 1) * P * PACK, :].rearrange("(p i) r -> p i r", i=PACK))
+            down_raw.append(raw)
+        table1 = slots.tile([P, T], U32, name="table1", align_bytes=64, offset=slot_c)
+        nc.sync.dma_start(table1[:].bitcast(I32), tab_words[1].rearrange("p t i -> p (t i)").bitcast(I32))
+
         bias_rows = keep.tile([P, P], F32, name="bias_rows")
-        moved_plane = keep.tile([P, S], U8, name="moved_plane", align_bytes=64)
-        nc.vector.memset(tab_plane[:].bitcast(I32), 0)
-        nc.vector.memset(w4_plane[:].bitcast(I32), 0)
-        nc.vector.memset(bias_rows[:], 0.0)
-        nc.vector.memset(moved_plane[:].bitcast(I32), 0)
+        nc.gpsimd.memset(bias_rows[:], 0.0)
+        nc.sync.dma_start(bias_rows[0:ROW_TILES, :], b.rearrange("(n p) -> n p", p=P))
+
+        nc.vector.memset(tab_plane[32:64, :].bitcast(I32), 0)
+        nc.vector.memset(tab_plane[64:128, :].bitcast(I32), 0)
+        picked_plane = keep.tile([P, S], U8, name="picked_plane", align_bytes=64)
+        nc.vector.tensor_copy(picked_plane[:], tab_plane[:].indirect(offsets[:]))
+        word_plane = keep.tile([P, PASSES, S], U8, name="word_plane", align_bytes=64)
+        nc.gpsimd.memset(word_plane[:].bitcast(I32), 0)
         for q in range(4):
-            nc.gpsimd.dma_start(
-                tab_plane[32 * q : 32 * q + 4 * PASSES, :].bitcast(I32),
-                tab_scales[:, 4 * q : 4 * q + 4, :].bitcast(I32),
+            nc.sync.dma_start(
+                word_plane[32 * q : 32 * q + 4, :, :].bitcast(I32),
+                picked_plane[8 * q : 8 * q + 8, :].bitcast(I32),
             )
+
+        up_raw = slots.tile([P, PACK, M], F32, name="up_raw", align_bytes=64, offset=slot_d)
+        nc.sync.dma_start(up_raw[:], up.rearrange("(p i) n -> p i n", i=PACK))
+        w4_codes = slots.tile([P, PASSES, 2 * M], U8, name="w4_codes", align_bytes=64, offset=w4_at)
+        nc.sync.dma_start(w4_codes[:].bitcast(I32), w4_words.rearrange("a p n -> p a n").bitcast(I32))
+        w4_plane = slots.tile([P, PASSES, M], U8, name="w4_plane", align_bytes=64, offset=w4_plane_at)
+        nc.vector.memset(w4_plane[:].bitcast(I32), 0)
         for q in range(4):
-            nc.gpsimd.dma_start(
+            nc.sync.dma_start(
                 w4_plane[32 * q : 32 * q + 4, :, :].bitcast(I32),
                 w4_scales[:, 4 * q : 4 * q + 4, :].rearrange("a r n -> r a n").bitcast(I32),
             )
-        nc.gpsimd.dma_start(bias_rows[0:ROW_TILES, :], b.rearrange("(n p) -> n p", p=P))
+        residual = []
+
+        def load_residual(n):
+            rows = slots.tile([P, T], F32, name=f"residual{n}", align_bytes=64, offset=residual_slots[n % 5])
+            nc.sync.dma_start(rows[:], rT[n * P : (n + 1) * P, :])
+            residual.append(rows)
+
+        for n in range(4):
+            load_residual(n)
+
         identity = keep.tile([P, P], F32, name="identity")
         make_identity(nc, identity[:])
         bias_bank = psum_h.tile([P, PACK, P], F32, name="bias_bank", tag="h_bank")
@@ -93,32 +112,27 @@ def tile_list_tabres_silu_kernel(
         nc.scalar.copy(bias[:], bias_bank[:, 0, 0:ROW_TILES])
 
         words0 = keep.tile([P, S], U32, name="words0", align_bytes=64)
-        nc.vector.tensor_copy(words0[:], table[0][:].indirect(offsets[:]))
-        picked_plane = keep.tile([P, S], U8, name="picked_plane", align_bytes=64)
-        nc.vector.tensor_copy(picked_plane[:], tab_plane[:].indirect(offsets[:]))
-        for q in range(4):
-            nc.gpsimd.dma_start(
-                moved_plane[32 * q : 32 * q + 4, :].bitcast(I32),
-                picked_plane[32 * q + 4 : 32 * q + 8, :].bitcast(I32),
-            )
+        nc.vector.tensor_copy(words0[:], table0[:].indirect(offsets[:]))
 
         down_codes, down_plane = [], []
         for a in range(PASSES):
-            grouped = stage.tile([P, PACK * R], BF16, name=f"down_bf16_{a}", tag="grouped", align_bytes=64)
+            grouped = slots.tile(
+                [P, PACK * R], BF16, name=f"down_bf16_{a}", align_bytes=64, offset=slot_e + a * SLOT // 4
+            )
             nc.scalar.copy(
                 grouped[:].rearrange("p (t m i) -> p m t i", t=PACK, i=PACK),
-                down_raw[:, a].rearrange("p i (m t) -> p m t i", t=PACK),
+                down_raw[a][:].rearrange("p i (m t) -> p m t i", t=PACK),
             )
             codes = keep.tile([P, R], U32, name=f"down_codes{a}", align_bytes=64)
-            plane = reused.tile([P, R], U8, name=f"down_plane{a}", align_bytes=64, offset=8192 + a * R)
+            plane = keep.tile([P, R], U8, name=f"down_plane{a}", align_bytes=64)
             nc.vector.quantize_mx(out=codes[:].bitcast(FP8X4), scales=plane[:], in_=grouped[:])
             down_codes.append(codes)
             down_plane.append(plane)
 
-        words1 = reused.tile([P, S], U32, name="words1", align_bytes=64, offset=0)
+        words1 = keep.tile([P, S], U32, name="words1", align_bytes=64)
         for c in range(CHUNKS):
             nc.vector.tensor_copy(
-                words1[:, c * CHUNK : (c + 1) * CHUNK], table[1][:].indirect(picks(c * CHUNK, CHUNK))
+                words1[:, c * CHUNK : (c + 1) * CHUNK], table1[:].indirect(picks(c * CHUNK, CHUNK))
             )
         words = [words0, words1]
 
@@ -126,18 +140,22 @@ def tile_list_tabres_silu_kernel(
             return words[a][:, first : first + count].bitcast(FP8X4)
 
         up_codes, up_plane = [], []
-        up_grouped = reused.tile([P, PACK * M], BF16, name="up_grouped", align_bytes=64, offset=8192 + PASSES * R)
         for half in range(M // CHUNK):
-            grouped = up_grouped[:, half * PACK * CHUNK : (half + 1) * PACK * CHUNK]
+            grouped = slots.tile(
+                [P, PACK * CHUNK], BF16, name=f"up_bf16_{half}", align_bytes=64, offset=slot_e + (2 + half) * SLOT // 4
+            )
             nc.vector.tensor_copy(
-                grouped.rearrange("p (c e i) -> p c i e", e=4, i=PACK),
+                grouped[:].rearrange("p (c e i) -> p c i e", e=4, i=PACK),
                 up_raw[:, :, half * CHUNK : (half + 1) * CHUNK].rearrange("p i (c e) -> p c i e", e=4),
             )
             codes = keep.tile([P, CHUNK], U32, name=f"up_codes{half}", align_bytes=64)
             plane = keep.tile([P, CHUNK], U8, name=f"up_plane{half}", align_bytes=64)
-            nc.vector.quantize_mx(out=codes[:].bitcast(FP8X4), scales=plane[:], in_=grouped)
+            nc.vector.quantize_mx(out=codes[:].bitcast(FP8X4), scales=plane[:], in_=grouped[:])
             up_codes.append(codes)
             up_plane.append(plane)
+
+        for n in range(4, ROW_TILES):
+            load_residual(n)
 
         h_codes, h_plane = [], []
         for c in range(CHUNKS):
@@ -152,7 +170,7 @@ def tile_list_tabres_silu_kernel(
                             lhsT=down_codes[a][:, t * P : (t + 1) * P].bitcast(FP8X4),
                             lhsT_scale=down_plane[a][:, t * P : (t + 1) * P],
                             rhs=moving_words(a, first, P),
-                            rhs_scale=picked_plane[4 * a :, first : first + P],
+                            rhs_scale=word_plane[:, a, first : first + P],
                             start=(a == 0),
                             stop=(a == PASSES - 1),
                         )
@@ -166,7 +184,6 @@ def tile_list_tabres_silu_kernel(
             h_codes.append(codes)
             h_plane.append(plane)
 
-        word_planes = [picked_plane, moved_plane]
         for n in range(ROW_TILES):
             half, within = divmod(n * P, CHUNK)
             result = outs.tile([P, S], F32, name=f"result{n}", tag="result")
@@ -182,7 +199,7 @@ def tile_list_tabres_silu_kernel(
                             lhsT=w4_codes[:, a, 2 * n * P : 2 * (n + 1) * P].bitcast(FP4X4),
                             lhsT_scale=w4_plane[:, a, n * P : (n + 1) * P],
                             rhs=moving_words(a, c * CHUNK, CHUNK),
-                            rhs_scale=word_planes[a][:, cols],
+                            rhs_scale=word_plane[:, a, cols],
                             start=(a == 0),
                             stop=False,
                         )

@@ -39,8 +39,7 @@ def tile_list_tabres_silu_kernel(
         stage = ctx.enter_context(tc.tile_pool(name="stage", bufs=3))
         acts = ctx.enter_context(tc.tile_pool(name="acts", bufs=4))
         outs = ctx.enter_context(tc.tile_pool(name="outs", bufs=OUT_BUFS))
-        psum_h = ctx.enter_context(tc.psum_pool(name="psum_h", bufs=4))
-        psum_y = ctx.enter_context(tc.psum_pool(name="psum_y", bufs=4))
+        psum = ctx.enter_context(tc.psum_pool(name="psum", bufs=8))
 
         offsets = keep.tile([P, S // LIST_ROWS], U16, name="offsets")
         nc.sync.dma_start(offsets[:], offs)
@@ -48,11 +47,12 @@ def tile_list_tabres_silu_kernel(
         def picks(first, count):
             return offsets[:, first // LIST_ROWS : (first + count) // LIST_ROWS]
 
-        slot_a, slot_b, slot_c, slot_e = 0, SLOT, 2 * SLOT, 3 * SLOT
-        w4_at = 4 * SLOT
-        w4_plane_at = w4_at + 4096
-        slot_d = w4_plane_at + 2048
+        slot_a, slot_b, slot_e, slot_c = 0, SLOT, 2 * SLOT, 3 * SLOT
+        w4_plane_at = 4 * SLOT
         window_at = w4_plane_at - 1024
+        w4_at = w4_plane_at + 3072
+        picked_at = w4_at + 3072
+        slot_d = w4_at + 4096
         residual_slots = [slot_a, slot_b, slot_c, slot_d, slot_e]
 
         tab_plane = slots.tile([P, T], U8, name="tab_plane", align_bytes=64, offset=window_at)
@@ -64,16 +64,18 @@ def tile_list_tabres_silu_kernel(
             raw = slots.tile([P, PACK, R], F32, name=f"down_raw{a}", align_bytes=64, offset=slot_b + a * SLOT // 2)
             nc.sync.dma_start(raw[:], down[a * P * PACK : (a + 1) * P * PACK, :].rearrange("(p i) r -> p i r", i=PACK))
             down_raw.append(raw)
-        table1 = slots.tile([P, T], U32, name="table1", align_bytes=64, offset=slot_c)
-        nc.sync.dma_start(table1[:].bitcast(I32), tab_words[1].rearrange("p t i -> p (t i)").bitcast(I32))
 
+        warm_in = keep.tile([P, 1], F32, name="warm_in")
+        warm_out = keep.tile([P, 1], F32, name="warm_out")
+        nc.gpsimd.memset(warm_in[:], 0.0)
+        nc.scalar.activation(warm_out[:], warm_in[:], ACT.Silu)
         bias_rows = keep.tile([P, P], F32, name="bias_rows")
         nc.gpsimd.memset(bias_rows[:], 0.0)
         nc.sync.dma_start(bias_rows[0:ROW_TILES, :], b.rearrange("(n p) -> n p", p=P))
 
         nc.vector.memset(tab_plane[32:64, :].bitcast(I32), 0)
         nc.vector.memset(tab_plane[64:128, :].bitcast(I32), 0)
-        picked_plane = keep.tile([P, S], U8, name="picked_plane", align_bytes=64)
+        picked_plane = slots.tile([P, S], U8, name="picked_plane", align_bytes=64, offset=picked_at)
         nc.vector.tensor_copy(picked_plane[:], tab_plane[:].indirect(offsets[:]))
         word_plane = keep.tile([P, PASSES, S], U8, name="word_plane", align_bytes=64)
         nc.gpsimd.memset(word_plane[:].bitcast(I32), 0)
@@ -83,6 +85,8 @@ def tile_list_tabres_silu_kernel(
                 picked_plane[8 * q : 8 * q + 8, :].bitcast(I32),
             )
 
+        table1 = slots.tile([P, T], U32, name="table1", align_bytes=64, offset=slot_c)
+        nc.sync.dma_start(table1[:].bitcast(I32), tab_words[1].rearrange("p t i -> p (t i)").bitcast(I32))
         up_raw = slots.tile([P, PACK, M], F32, name="up_raw", align_bytes=64, offset=slot_d)
         nc.sync.dma_start(up_raw[:], up.rearrange("(p i) n -> p i n", i=PACK))
         w4_codes = slots.tile([P, PASSES, 2 * M], U8, name="w4_codes", align_bytes=64, offset=w4_at)
@@ -106,10 +110,10 @@ def tile_list_tabres_silu_kernel(
 
         identity = keep.tile([P, P], F32, name="identity")
         make_identity(nc, identity[:])
-        bias_bank = psum_h.tile([P, PACK, P], F32, name="bias_bank", tag="h_bank")
-        nc.tensor.transpose(bias_bank[:, 0, :], bias_rows[:], identity[:])
+        bias_bank = psum.tile([P, CHUNK], F32, name="bias_bank", tag="bank")
+        nc.tensor.transpose(bias_bank[:, 0:P], bias_rows[:], identity[:])
         bias = keep.tile([P, ROW_TILES], F32, name="bias")
-        nc.scalar.copy(bias[:], bias_bank[:, 0, 0:ROW_TILES])
+        nc.scalar.copy(bias[:], bias_bank[:, 0:ROW_TILES])
 
         words0 = keep.tile([P, S], U32, name="words0", align_bytes=64)
         nc.vector.tensor_copy(words0[:], table0[:].indirect(offsets[:]))
@@ -158,25 +162,26 @@ def tile_list_tabres_silu_kernel(
             load_residual(n)
 
         h_codes, h_plane = [], []
-        for c in range(CHUNKS):
+
+        def low_rank_chunk(c):
             grouped = stage.tile([P, PACK * CHUNK], BF16, name=f"h_bf16_{c}", tag="grouped", align_bytes=64)
             for block in range(CHUNK // P):
                 first = c * CHUNK + block * P
-                bank = psum_h.tile([P, PACK, P], F32, name=f"h_bank{c}_{block}", tag="h_bank")
-                for t in range(PACK):
-                    for a in range(PASSES):
+                bank = psum.tile([P, CHUNK], F32, name=f"h_bank{c}_{block}", tag="bank")
+                for a in range(PASSES):
+                    for t in range(PACK):
                         nc.tensor.matmul_mx(
-                            out=bank[:, t, :],
+                            out=bank[:, t * P : (t + 1) * P],
                             lhsT=down_codes[a][:, t * P : (t + 1) * P].bitcast(FP8X4),
                             lhsT_scale=down_plane[a][:, t * P : (t + 1) * P],
                             rhs=moving_words(a, first, P),
                             rhs_scale=word_plane[:, a, first : first + P],
-                            start=(a == 0),
-                            stop=(a == PASSES - 1),
+                            start=(a == 0 and t == 0),
+                            stop=(a == PASSES - 1 and t == PACK - 1),
                         )
                 nc.scalar.copy(
                     grouped[:, block * P * PACK : (block + 1) * P * PACK].rearrange("p (j t) -> p j t", t=PACK),
-                    bank[:].rearrange("p t j -> p j t"),
+                    bank[:].rearrange("p (t j) -> p j t", t=PACK),
                 )
             codes = keep.tile([P, CHUNK], U32, name=f"h_codes{c}", align_bytes=64)
             plane = keep.tile([P, CHUNK], U8, name=f"h_plane{c}", align_bytes=64)
@@ -184,41 +189,55 @@ def tile_list_tabres_silu_kernel(
             h_codes.append(codes)
             h_plane.append(plane)
 
-        for n in range(ROW_TILES):
+        results = {}
+
+        def output_piece(n, first, count):
             half, within = divmod(n * P, CHUNK)
-            result = outs.tile([P, S], F32, name=f"result{n}", tag="result")
-            for piece in range(S // PIECE):
-                activated = acts.tile([P, PIECE], F32, name=f"silu{n}_{piece}", tag="silu")
-                for cc in range(PIECE // CHUNK):
-                    c = piece * (PIECE // CHUNK) + cc
-                    cols = slice(c * CHUNK, (c + 1) * CHUNK)
-                    bank = psum_y.tile([P, CHUNK], F32, name=f"y_bank{n}_{c}", tag="y_bank")
-                    for a in range(PASSES):
-                        nc.tensor.matmul_mx(
-                            out=bank[:],
-                            lhsT=w4_codes[:, a, 2 * n * P : 2 * (n + 1) * P].bitcast(FP4X4),
-                            lhsT_scale=w4_plane[:, a, n * P : (n + 1) * P],
-                            rhs=moving_words(a, c * CHUNK, CHUNK),
-                            rhs_scale=word_plane[:, a, cols],
-                            start=(a == 0),
-                            stop=False,
-                        )
+            if n not in results:
+                results[n] = outs.tile([P, S], F32, name=f"result{n}", tag="result")
+            activated = acts.tile([P, count], F32, name=f"silu{n}_{first}", tag="silu")
+            for c in range(first // CHUNK, (first + count) // CHUNK):
+                cols = slice(c * CHUNK, (c + 1) * CHUNK)
+                bank = psum.tile([P, CHUNK], F32, name=f"y_bank{n}_{c}", tag="bank")
+                for a in range(PASSES):
                     nc.tensor.matmul_mx(
                         out=bank[:],
-                        lhsT=up_codes[half][:, within : within + P].bitcast(FP8X4),
-                        lhsT_scale=up_plane[half][:, within : within + P],
-                        rhs=h_codes[c][:].bitcast(FP8X4),
-                        rhs_scale=h_plane[c][:],
-                        start=False,
-                        stop=True,
+                        lhsT=w4_codes[:, a, 2 * n * P : 2 * (n + 1) * P].bitcast(FP4X4),
+                        lhsT_scale=w4_plane[:, a, n * P : (n + 1) * P],
+                        rhs=moving_words(a, c * CHUNK, CHUNK),
+                        rhs_scale=word_plane[:, a, cols],
+                        start=(a == 0),
+                        stop=False,
                     )
-                    nc.scalar.activation(
-                        activated[:, cc * CHUNK : (cc + 1) * CHUNK], bank[:], ACT.Silu, bias=bias[:, n : n + 1]
-                    )
-                nc.vector.tensor_tensor(
-                    result[:, piece * PIECE : (piece + 1) * PIECE],
-                    residual[n][:].indirect(picks(piece * PIECE, PIECE)),
-                    activated[:],
-                    ADD,
+                nc.tensor.matmul_mx(
+                    out=bank[:],
+                    lhsT=up_codes[half][:, within : within + P].bitcast(FP8X4),
+                    lhsT_scale=up_plane[half][:, within : within + P],
+                    rhs=h_codes[c][:].bitcast(FP8X4),
+                    rhs_scale=h_plane[c][:],
+                    start=False,
+                    stop=True,
                 )
-            nc.sync.dma_start(out[n * P : (n + 1) * P, :], result[:])
+                nc.scalar.activation(
+                    activated[:, c * CHUNK - first : (c + 1) * CHUNK - first], bank[:], ACT.Silu, bias=bias[:, n : n + 1]
+                )
+            nc.vector.tensor_tensor(
+                results[n][:, first : first + count],
+                residual[n][:].indirect(picks(first, count)),
+                activated[:],
+                ADD,
+            )
+
+        def store(n, first, count):
+            nc.sync.dma_start(out[n * P : (n + 1) * P, first : first + count], results[n][:, first : first + count])
+
+        for c in range(CHUNKS):
+            low_rank_chunk(c)
+        for n in range(ROW_TILES - 1):
+            output_piece(n, 0, PIECE)
+            output_piece(n, PIECE, PIECE)
+            store(n, 0, S)
+        last = ROW_TILES - 1
+        for first, count in ((0, PIECE), (PIECE, CHUNK), (PIECE + CHUNK, CHUNK)):
+            output_piece(last, first, count)
+            store(last, first, count)

@@ -20,13 +20,23 @@ ADD = mybir.AluOpType.add
 P = 128
 PACK = 4
 PASSES = K // (P * PACK)
+QUADRANT = 32
+PLANE_ROWS = 4
+SCALE_ROWS = PASSES * P // 8
+LINE = 4
 CHUNK = 512
 CHUNKS = S // CHUNK
 ROW_TILES = M // P
 PIECE = 1024
 LIST_ROWS = 16
+ALIGN = 64
+
 SLOT = 4 * T
+SLOTS = 5
+H_BUFS = 3
+SILU_BUFS = 4
 OUT_BUFS = 6
+BANKS = 8
 
 
 def tile_list_tabres_silu_kernel(
@@ -36,10 +46,10 @@ def tile_list_tabres_silu_kernel(
     with ExitStack() as ctx:
         keep = ctx.enter_context(tc.tile_pool(name="keep", bufs=1))
         slots = ctx.enter_context(tc.tile_pool(name="slots", bufs=1))
-        stage = ctx.enter_context(tc.tile_pool(name="stage", bufs=3))
-        acts = ctx.enter_context(tc.tile_pool(name="acts", bufs=4))
+        stage = ctx.enter_context(tc.tile_pool(name="stage", bufs=H_BUFS))
+        acts = ctx.enter_context(tc.tile_pool(name="acts", bufs=SILU_BUFS))
         outs = ctx.enter_context(tc.tile_pool(name="outs", bufs=OUT_BUFS))
-        psum = ctx.enter_context(tc.psum_pool(name="psum", bufs=8))
+        psum = ctx.enter_context(tc.psum_pool(name="psum", bufs=BANKS))
 
         offsets = keep.tile([P, S // LIST_ROWS], U16, name="offsets")
         nc.sync.dma_start(offsets[:], offs)
@@ -49,63 +59,68 @@ def tile_list_tabres_silu_kernel(
 
         slot_a, slot_b, slot_e, slot_c = 0, SLOT, 2 * SLOT, 3 * SLOT
         w4_plane_at = 4 * SLOT
-        window_at = w4_plane_at - 1024
-        w4_at = w4_plane_at + 3072
-        picked_at = w4_at + 3072
-        slot_d = w4_at + 4096
+        window_at = w4_plane_at - T // 4
+        w4_at = window_at + T
+        slot_d = w4_at + PASSES * 2 * M
+        picked_at = slot_d - S // 2
         residual_slots = [slot_a, slot_b, slot_c, slot_d, slot_e]
 
-        tab_plane = slots.tile([P, T], U8, name="tab_plane", align_bytes=64, offset=window_at)
-        nc.sync.dma_start(tab_plane[0:32, :].bitcast(I32), tab_scales.rearrange("a q t -> q a t").bitcast(I32))
-        table0 = slots.tile([P, T], U32, name="table0", align_bytes=64, offset=slot_a)
+        scale_window = slots.tile([P, T], U8, name="scale_window", align_bytes=ALIGN, offset=window_at)
+        for a in range(PASSES):
+            nc.sync.dma_start(
+                scale_window[a:SCALE_ROWS:PASSES, :].bitcast(I32),
+                tab_scales[a].rearrange("(q s) t -> s q t", s=PLANE_ROWS).bitcast(I32),
+            )
+        table0 = slots.tile([P, T], U32, name="table0", align_bytes=ALIGN, offset=slot_a)
         nc.sync.dma_start(table0[:].bitcast(I32), tab_words[0].rearrange("p t i -> p (t i)").bitcast(I32))
         down_raw = []
         for a in range(PASSES):
-            raw = slots.tile([P, PACK, R], F32, name=f"down_raw{a}", align_bytes=64, offset=slot_b + a * SLOT // 2)
+            raw = slots.tile(
+                [P, PACK, R], F32, name=f"down_raw{a}", align_bytes=ALIGN, offset=slot_b + a * SLOT // PASSES
+            )
             nc.sync.dma_start(raw[:], down[a * P * PACK : (a + 1) * P * PACK, :].rearrange("(p i) r -> p i r", i=PACK))
             down_raw.append(raw)
 
-        warm_in = keep.tile([P, 1], F32, name="warm_in")
-        warm_out = keep.tile([P, 1], F32, name="warm_out")
-        nc.gpsimd.memset(warm_in[:], 0.0)
-        nc.scalar.activation(warm_out[:], warm_in[:], ACT.Silu)
         bias_rows = keep.tile([P, P], F32, name="bias_rows")
         nc.gpsimd.memset(bias_rows[:], 0.0)
         nc.sync.dma_start(bias_rows[0:ROW_TILES, :], b.rearrange("(n p) -> n p", p=P))
 
-        nc.vector.memset(tab_plane[32:64, :].bitcast(I32), 0)
-        nc.vector.memset(tab_plane[64:128, :].bitcast(I32), 0)
-        picked_plane = slots.tile([P, S], U8, name="picked_plane", align_bytes=64, offset=picked_at)
-        nc.vector.tensor_copy(picked_plane[:], tab_plane[:].indirect(offsets[:]))
-        word_plane = keep.tile([P, PASSES, S], U8, name="word_plane", align_bytes=64)
+        nc.vector.memset(scale_window[SCALE_ROWS : P // 2, :].bitcast(I32), 0)
+        nc.vector.memset(scale_window[P // 2 : P, :].bitcast(I32), 0)
+        picked_rows = slots.tile([P, S], U8, name="picked_rows", align_bytes=ALIGN, offset=picked_at)
+        nc.vector.tensor_copy(picked_rows[:], scale_window[:].indirect(offsets[:]))
+
+        word_plane = keep.tile([P, PASSES, S], U8, name="word_plane", align_bytes=ALIGN)
         nc.gpsimd.memset(word_plane[:].bitcast(I32), 0)
-        for q in range(4):
+        rows_per_move = SCALE_ROWS // PLANE_ROWS
+        for s in range(PLANE_ROWS):
             nc.sync.dma_start(
-                word_plane[32 * q : 32 * q + 4, :, :].bitcast(I32),
-                picked_plane[8 * q : 8 * q + 8, :].bitcast(I32),
+                word_plane[s:P:QUADRANT, :, :].bitcast(I32),
+                picked_rows[rows_per_move * s : rows_per_move * (s + 1), :].bitcast(I32),
             )
 
-        table1 = slots.tile([P, T], U32, name="table1", align_bytes=64, offset=slot_c)
+        table1 = slots.tile([P, T], U32, name="table1", align_bytes=ALIGN, offset=slot_c)
         nc.sync.dma_start(table1[:].bitcast(I32), tab_words[1].rearrange("p t i -> p (t i)").bitcast(I32))
-        up_raw = slots.tile([P, PACK, M], F32, name="up_raw", align_bytes=64, offset=slot_d)
+        up_raw = slots.tile([P, PACK, M], F32, name="up_raw", align_bytes=ALIGN, offset=slot_d)
         nc.sync.dma_start(up_raw[:], up.rearrange("(p i) n -> p i n", i=PACK))
-        w4_codes = slots.tile([P, PASSES, 2 * M], U8, name="w4_codes", align_bytes=64, offset=w4_at)
+        w4_codes = slots.tile([P, PASSES, 2 * M], U8, name="w4_codes", align_bytes=ALIGN, offset=w4_at)
         nc.sync.dma_start(w4_codes[:].bitcast(I32), w4_words.rearrange("a p n -> p a n").bitcast(I32))
-        w4_plane = slots.tile([P, PASSES, M], U8, name="w4_plane", align_bytes=64, offset=w4_plane_at)
+        w4_plane = slots.tile([P, PASSES, M], U8, name="w4_plane", align_bytes=ALIGN, offset=w4_plane_at)
         nc.vector.memset(w4_plane[:].bitcast(I32), 0)
-        for q in range(4):
+        for s in range(PLANE_ROWS):
             nc.sync.dma_start(
-                w4_plane[32 * q : 32 * q + 4, :, :].bitcast(I32),
-                w4_scales[:, 4 * q : 4 * q + 4, :].rearrange("a r n -> r a n").bitcast(I32),
+                w4_plane[s:P:QUADRANT, :, :].bitcast(I32),
+                w4_scales[:, s : SCALE_ROWS // PASSES : PLANE_ROWS, :].rearrange("a q n -> q a n").bitcast(I32),
             )
+
         residual = []
 
         def load_residual(n):
-            rows = slots.tile([P, T], F32, name=f"residual{n}", align_bytes=64, offset=residual_slots[n % 5])
+            rows = slots.tile([P, T], F32, name=f"residual{n}", align_bytes=ALIGN, offset=residual_slots[n % SLOTS])
             nc.sync.dma_start(rows[:], rT[n * P : (n + 1) * P, :])
             residual.append(rows)
 
-        for n in range(4):
+        for n in range(SLOTS - 1):
             load_residual(n)
 
         identity = keep.tile([P, P], F32, name="identity")
@@ -115,25 +130,25 @@ def tile_list_tabres_silu_kernel(
         bias = keep.tile([P, ROW_TILES], F32, name="bias")
         nc.scalar.copy(bias[:], bias_bank[:, 0:ROW_TILES])
 
-        words0 = keep.tile([P, S], U32, name="words0", align_bytes=64)
+        words0 = keep.tile([P, S], U32, name="words0", align_bytes=ALIGN)
         nc.vector.tensor_copy(words0[:], table0[:].indirect(offsets[:]))
 
         down_codes, down_plane = [], []
         for a in range(PASSES):
             grouped = slots.tile(
-                [P, PACK * R], BF16, name=f"down_bf16_{a}", align_bytes=64, offset=slot_e + a * SLOT // 4
+                [P, PACK * R], BF16, name=f"down_bf16_{a}", align_bytes=ALIGN, offset=slot_e + a * SLOT // 4
             )
             nc.scalar.copy(
                 grouped[:].rearrange("p (t m i) -> p m t i", t=PACK, i=PACK),
                 down_raw[a][:].rearrange("p i (m t) -> p m t i", t=PACK),
             )
-            codes = keep.tile([P, R], U32, name=f"down_codes{a}", align_bytes=64)
-            plane = keep.tile([P, R], U8, name=f"down_plane{a}", align_bytes=64)
+            codes = keep.tile([P, R], U32, name=f"down_codes{a}", align_bytes=ALIGN)
+            plane = keep.tile([P, R], U8, name=f"down_plane{a}", align_bytes=ALIGN)
             nc.vector.quantize_mx(out=codes[:].bitcast(FP8X4), scales=plane[:], in_=grouped[:])
             down_codes.append(codes)
             down_plane.append(plane)
 
-        words1 = keep.tile([P, S], U32, name="words1", align_bytes=64)
+        words1 = keep.tile([P, S], U32, name="words1", align_bytes=ALIGN)
         for c in range(CHUNKS):
             nc.vector.tensor_copy(
                 words1[:, c * CHUNK : (c + 1) * CHUNK], table1[:].indirect(picks(c * CHUNK, CHUNK))
@@ -146,25 +161,28 @@ def tile_list_tabres_silu_kernel(
         up_codes, up_plane = [], []
         for half in range(M // CHUNK):
             grouped = slots.tile(
-                [P, PACK * CHUNK], BF16, name=f"up_bf16_{half}", align_bytes=64, offset=slot_e + (2 + half) * SLOT // 4
+                [P, PACK * CHUNK],
+                BF16,
+                name=f"up_bf16_{half}",
+                align_bytes=ALIGN,
+                offset=slot_e + (PASSES + half) * SLOT // 4,
             )
             nc.vector.tensor_copy(
-                grouped[:].rearrange("p (c e i) -> p c i e", e=4, i=PACK),
-                up_raw[:, :, half * CHUNK : (half + 1) * CHUNK].rearrange("p i (c e) -> p c i e", e=4),
+                grouped[:].rearrange("p (c e i) -> p c i e", e=LINE, i=PACK),
+                up_raw[:, :, half * CHUNK : (half + 1) * CHUNK].rearrange("p i (c e) -> p c i e", e=LINE),
             )
-            codes = keep.tile([P, CHUNK], U32, name=f"up_codes{half}", align_bytes=64)
-            plane = keep.tile([P, CHUNK], U8, name=f"up_plane{half}", align_bytes=64)
+            codes = keep.tile([P, CHUNK], U32, name=f"up_codes{half}", align_bytes=ALIGN)
+            plane = keep.tile([P, CHUNK], U8, name=f"up_plane{half}", align_bytes=ALIGN)
             nc.vector.quantize_mx(out=codes[:].bitcast(FP8X4), scales=plane[:], in_=grouped[:])
             up_codes.append(codes)
             up_plane.append(plane)
 
-        for n in range(4, ROW_TILES):
+        for n in range(SLOTS - 1, ROW_TILES):
             load_residual(n)
 
         h_codes, h_plane = [], []
-
-        def low_rank_chunk(c):
-            grouped = stage.tile([P, PACK * CHUNK], BF16, name=f"h_bf16_{c}", tag="grouped", align_bytes=64)
+        for c in range(CHUNKS):
+            grouped = stage.tile([P, PACK * CHUNK], BF16, name=f"h_bf16_{c}", tag="grouped", align_bytes=ALIGN)
             for block in range(CHUNK // P):
                 first = c * CHUNK + block * P
                 bank = psum.tile([P, CHUNK], F32, name=f"h_bank{c}_{block}", tag="bank")
@@ -183,18 +201,14 @@ def tile_list_tabres_silu_kernel(
                     grouped[:, block * P * PACK : (block + 1) * P * PACK].rearrange("p (j t) -> p j t", t=PACK),
                     bank[:].rearrange("p (t j) -> p j t", t=PACK),
                 )
-            codes = keep.tile([P, CHUNK], U32, name=f"h_codes{c}", align_bytes=64)
-            plane = keep.tile([P, CHUNK], U8, name=f"h_plane{c}", align_bytes=64)
+            codes = keep.tile([P, CHUNK], U32, name=f"h_codes{c}", align_bytes=ALIGN)
+            plane = keep.tile([P, CHUNK], U8, name=f"h_plane{c}", align_bytes=ALIGN)
             nc.vector.quantize_mx(out=codes[:].bitcast(FP8X4), scales=plane[:], in_=grouped[:])
             h_codes.append(codes)
             h_plane.append(plane)
 
-        results = {}
-
-        def output_piece(n, first, count):
+        def output_piece(result, n, first, count):
             half, within = divmod(n * P, CHUNK)
-            if n not in results:
-                results[n] = outs.tile([P, S], F32, name=f"result{n}", tag="result")
             activated = acts.tile([P, count], F32, name=f"silu{n}_{first}", tag="silu")
             for c in range(first // CHUNK, (first + count) // CHUNK):
                 cols = slice(c * CHUNK, (c + 1) * CHUNK)
@@ -222,22 +236,22 @@ def tile_list_tabres_silu_kernel(
                     activated[:, c * CHUNK - first : (c + 1) * CHUNK - first], bank[:], ACT.Silu, bias=bias[:, n : n + 1]
                 )
             nc.vector.tensor_tensor(
-                results[n][:, first : first + count],
+                result[:, first : first + count],
                 residual[n][:].indirect(picks(first, count)),
                 activated[:],
                 ADD,
             )
 
-        def store(n, first, count):
-            nc.sync.dma_start(out[n * P : (n + 1) * P, first : first + count], results[n][:, first : first + count])
+        def store(result, n, first, count):
+            nc.sync.dma_start(out[n * P : (n + 1) * P, first : first + count], result[:, first : first + count])
 
-        for c in range(CHUNKS):
-            low_rank_chunk(c)
-        for n in range(ROW_TILES - 1):
-            output_piece(n, 0, PIECE)
-            output_piece(n, PIECE, PIECE)
-            store(n, 0, S)
         last = ROW_TILES - 1
+        for n in range(last):
+            result = outs.tile([P, S], F32, name=f"result{n}", tag="result")
+            for first in range(0, S, PIECE):
+                output_piece(result, n, first, PIECE)
+            store(result, n, 0, S)
+        result = outs.tile([P, S], F32, name=f"result{last}", tag="result")
         for first, count in ((0, PIECE), (PIECE, CHUNK), (PIECE + CHUNK, CHUNK)):
-            output_piece(last, first, count)
-            store(last, first, count)
+            output_piece(result, last, first, count)
+            store(result, last, first, count)

@@ -37,6 +37,7 @@ H_BUFS = 3
 SILU_BUFS = 4
 OUT_BUFS = 6
 BANKS = 8
+VECTOR_BLOCKS = 3
 
 
 def tile_list_tabres_silu_kernel(
@@ -197,7 +198,8 @@ def tile_list_tabres_silu_kernel(
                             start=(a == 0 and t == 0),
                             stop=(a == PASSES - 1 and t == PACK - 1),
                         )
-                nc.scalar.copy(
+                copy_out = nc.vector.tensor_copy if first >= S - VECTOR_BLOCKS * P else nc.scalar.copy
+                copy_out(
                     grouped[:, block * P * PACK : (block + 1) * P * PACK].rearrange("p (j t) -> p j t", t=PACK),
                     bank[:].rearrange("p (t j) -> p j t", t=PACK),
                 )

from contextlib import ExitStack

import concourse.mybir as mybir
from concourse.masks import make_identity

K, M, T, S, R = 1024, 1024, 4096, 2048, 512
FLOPS = 2 * S * (K * R + K * M + R * M)

F32 = mybir.dt.float32
BF16 = mybir.dt.bfloat16
I32 = mybir.dt.int32
U32 = mybir.dt.uint32
U16 = mybir.dt.uint16
U8 = mybir.dt.uint8
FP8X4 = mybir.dt.float8_e4m3fn_x4
FP4X4 = mybir.dt.float4_e2m1fn_x4
ACT = mybir.ActivationFunctionType
ADD = mybir.AluOpType.add

P = 128
PACK = 4
PASSES = K // (P * PACK)
QUADRANT = 32
PLANE_ROWS = 4
SCALE_ROWS = PASSES * P // 8
LINE = 4
CHUNK = 512
CHUNKS = S // CHUNK
ROW_TILES = M // P
PIECE = 1024
LIST_ROWS = 16
ALIGN = 64

SLOT = 4 * T
SLOTS = 5
H_BUFS = 3
SILU_BUFS = 4
OUT_BUFS = 6
BANKS = 8
VECTOR_BLOCKS = 3


def tile_list_tabres_silu_kernel(
    tc, tab_words, tab_scales, w4_words, w4_scales, down, up, rT, b, offs, out
):
    nc = tc.nc
    with ExitStack() as ctx:
        keep = ctx.enter_context(tc.tile_pool(name="keep", bufs=1))
        slots = ctx.enter_context(tc.tile_pool(name="slots", bufs=1))
        stage = ctx.enter_context(tc.tile_pool(name="stage", bufs=H_BUFS))
        acts = ctx.enter_context(tc.tile_pool(name="acts", bufs=SILU_BUFS))
        outs = ctx.enter_context(tc.tile_pool(name="outs", bufs=OUT_BUFS))
        psum = ctx.enter_context(tc.psum_pool(name="psum", bufs=BANKS))

        offsets = keep.tile([P, S // LIST_ROWS], U16, name="offsets")
        nc.sync.dma_start(offsets[:], offs)

        def picks(first, count):
            return offsets[:, first // LIST_ROWS : (first + count) // LIST_ROWS]

        slot_a, slot_b, slot_e, slot_c = 0, SLOT, 2 * SLOT, 3 * SLOT
        w4_plane_at = 4 * SLOT
        window_at = w4_plane_at - T // 4
        w4_at = window_at + T
        slot_d = w4_at + PASSES * 2 * M
        picked_at = slot_d - S // 2
        residual_slots = [slot_a, slot_b, slot_c, slot_d, slot_e]

        scale_window = slots.tile([P, T], U8, name="scale_window", align_bytes=ALIGN, offset=window_at)
        for a in range(PASSES):
            nc.sync.dma_start(
                scale_window[a:SCALE_ROWS:PASSES, :].bitcast(I32),
                tab_scales[a].rearrange("(q s) t -> s q t", s=PLANE_ROWS).bitcast(I32),
            )
        table0 = slots.tile([P, T], U32, name="table0", align_bytes=ALIGN, offset=slot_a)
        nc.sync.dma_start(table0[:].bitcast(I32), tab_words[0].rearrange("p t i -> p (t i)").bitcast(I32))
        down_raw = []
        for a in range(PASSES):
            raw = slots.tile(
                [P, PACK, R], F32, name=f"down_raw{a}", align_bytes=ALIGN, offset=slot_b + a * SLOT // PASSES
            )
            nc.sync.dma_start(raw[:], down[a * P * PACK : (a + 1) * P * PACK, :].rearrange("(p i) r -> p i r", i=PACK))
            down_raw.append(raw)

        bias_rows = keep.tile([P, P], F32, name="bias_rows")
        nc.gpsimd.memset(bias_rows[:], 0.0)
        nc.sync.dma_start(bias_rows[0:ROW_TILES, :], b.rearrange("(n p) -> n p", p=P))

        nc.vector.memset(scale_window[SCALE_ROWS : P // 2, :].bitcast(I32), 0)
        nc.vector.memset(scale_window[P // 2 : P, :].bitcast(I32), 0)
        picked_rows = slots.tile([P, S], U8, name="picked_rows", align_bytes=ALIGN, offset=picked_at)
        nc.vector.tensor_copy(picked_rows[:], scale_window[:].indirect(offsets[:]))

        word_plane = keep.tile([P, PASSES, S], U8, name="word_plane", align_bytes=ALIGN)
        nc.gpsimd.memset(word_plane[:].bitcast(I32), 0)
        rows_per_move = SCALE_ROWS // PLANE_ROWS
        for s in range(PLANE_ROWS):
            nc.sync.dma_start(
                word_plane[s:P:QUADRANT, :, :].bitcast(I32),
                picked_rows[rows_per_move * s : rows_per_move * (s + 1), :].bitcast(I32),
            )

        table1 = slots.tile([P, T], U32, name="table1", align_bytes=ALIGN, offset=slot_c)
        nc.sync.dma_start(table1[:].bitcast(I32), tab_words[1].rearrange("p t i -> p (t i)").bitcast(I32))
        up_raw = slots.tile([P, PACK, M], F32, name="up_raw", align_bytes=ALIGN, offset=slot_d)
        nc.sync.dma_start(up_raw[:], up.rearrange("(p i) n -> p i n", i=PACK))
        w4_codes = slots.tile([P, PASSES, 2 * M], U8, name="w4_codes", align_bytes=ALIGN, offset=w4_at)
        nc.sync.dma_start(w4_codes[:].bitcast(I32), w4_words.rearrange("a p n -> p a n").bitcast(I32))
        w4_plane = slots.tile([P, PASSES, M], U8, name="w4_plane", align_bytes=ALIGN, offset=w4_plane_at)
        nc.vector.memset(w4_plane[:].bitcast(I32), 0)
        for s in range(PLANE_ROWS):
            nc.sync.dma_start(
                w4_plane[s:P:QUADRANT, :, :].bitcast(I32),
                w4_scales[:, s : SCALE_ROWS // PASSES : PLANE_ROWS, :].rearrange("a q n -> q a n").bitcast(I32),
            )

        residual = []

        def load_residual(n):
            rows = slots.tile([P, T], F32, name=f"residual{n}", align_bytes=ALIGN, offset=residual_slots[n % SLOTS])
            nc.sync.dma_start(rows[:], rT[n * P : (n + 1) * P, :])
            residual.append(rows)

        for n in range(SLOTS - 1):
            load_residual(n)

        identity = keep.tile([P, P], F32, name="identity")
        make_identity(nc, identity[:])
        bias_bank = psum.tile([P, CHUNK], F32, name="bias_bank", tag="bank")
        nc.tensor.transpose(bias_bank[:, 0:P], bias_rows[:], identity[:])
        bias = keep.tile([P, ROW_TILES], F32, name="bias")
        nc.scalar.copy(bias[:], bias_bank[:, 0:ROW_TILES])

        words0 = keep.tile([P, S], U32, name="words0", align_bytes=ALIGN)
        nc.vector.tensor_copy(words0[:], table0[:].indirect(offsets[:]))

        down_codes, down_plane = [], []
        for a in range(PASSES):
            grouped = slots.tile(
                [P, PACK * R], BF16, name=f"down_bf16_{a}", align_bytes=ALIGN, offset=slot_e + a * SLOT // 4
            )
            nc.scalar.copy(
                grouped[:].rearrange("p (t m i) -> p m t i", t=PACK, i=PACK),
                down_raw[a][:].rearrange("p i (m t) -> p m t i", t=PACK),
            )
            codes = keep.tile([P, R], U32, name=f"down_codes{a}", align_bytes=ALIGN)
            plane = keep.tile([P, R], U8, name=f"down_plane{a}", align_bytes=ALIGN)
            nc.vector.quantize_mx(out=codes[:].bitcast(FP8X4), scales=plane[:], in_=grouped[:])
            down_codes.append(codes)
            down_plane.append(plane)

        words1 = keep.tile([P, S], U32, name="words1", align_bytes=ALIGN)
        for c in range(CHUNKS):
            nc.vector.tensor_copy(
                words1[:, c * CHUNK : (c + 1) * CHUNK], table1[:].indirect(picks(c * CHUNK, CHUNK))
            )
        words = [words0, words1]

        def moving_words(a, first, count):
            return words[a][:, first : first + count].bitcast(FP8X4)

        up_codes, up_plane = [], []
        for half in range(M // CHUNK):
            grouped = slots.tile(
                [P, PACK * CHUNK],
                BF16,
                name=f"up_bf16_{half}",
                align_bytes=ALIGN,
                offset=slot_e + (PASSES + half) * SLOT // 4,
            )
            nc.vector.tensor_copy(
                grouped[:].rearrange("p (c e i) -> p c i e", e=LINE, i=PACK),
                up_raw[:, :, half * CHUNK : (half + 1) * CHUNK].rearrange("p i (c e) -> p c i e", e=LINE),
            )
            codes = keep.tile([P, CHUNK], U32, name=f"up_codes{half}", align_bytes=ALIGN)
            plane = keep.tile([P, CHUNK], U8, name=f"up_plane{half}", align_bytes=ALIGN)
            nc.vector.quantize_mx(out=codes[:].bitcast(FP8X4), scales=plane[:], in_=grouped[:])
            up_codes.append(codes)
            up_plane.append(plane)

        for n in range(SLOTS - 1, ROW_TILES):
            load_residual(n)

        h_codes, h_plane = [], []
        for c in range(CHUNKS):
            grouped = stage.tile([P, PACK * CHUNK], BF16, name=f"h_bf16_{c}", tag="grouped", align_bytes=ALIGN)
            for block in range(CHUNK // P):
                first = c * CHUNK + block * P
                bank = psum.tile([P, CHUNK], F32, name=f"h_bank{c}_{block}", tag="bank")
                for a in range(PASSES):
                    for t in range(PACK):
                        nc.tensor.matmul_mx(
                            out=bank[:, t * P : (t + 1) * P],
                            lhsT=down_codes[a][:, t * P : (t + 1) * P].bitcast(FP8X4),
                            lhsT_scale=down_plane[a][:, t * P : (t + 1) * P],
                            rhs=moving_words(a, first, P),
                            rhs_scale=word_plane[:, a, first : first + P],
                            start=(a == 0 and t == 0),
                            stop=(a == PASSES - 1 and t == PACK - 1),
                        )
                copy_out = nc.vector.tensor_copy if first >= S - VECTOR_BLOCKS * P else nc.scalar.copy
                copy_out(
                    grouped[:, block * P * PACK : (block + 1) * P * PACK].rearrange("p (j t) -> p j t", t=PACK),
                    bank[:].rearrange("p (t j) -> p j t", t=PACK),
                )
            codes = keep.tile([P, CHUNK], U32, name=f"h_codes{c}", align_bytes=ALIGN)
            plane = keep.tile([P, CHUNK], U8, name=f"h_plane{c}", align_bytes=ALIGN)
            nc.vector.quantize_mx(out=codes[:].bitcast(FP8X4), scales=plane[:], in_=grouped[:])
            h_codes.append(codes)
            h_plane.append(plane)

        def output_piece(result, n, first, count):
            half, within = divmod(n * P, CHUNK)
            activated = acts.tile([P, count], F32, name=f"silu{n}_{first}", tag="silu")
            for c in range(first // CHUNK, (first + count) // CHUNK):
                cols = slice(c * CHUNK, (c + 1) * CHUNK)
                bank = psum.tile([P, CHUNK], F32, name=f"y_bank{n}_{c}", tag="bank")
                for a in range(PASSES):
                    nc.tensor.matmul_mx(
                        out=bank[:],
                        lhsT=w4_codes[:, a, 2 * n * P : 2 * (n + 1) * P].bitcast(FP4X4),
                        lhsT_scale=w4_plane[:, a, n * P : (n + 1) * P],
                        rhs=moving_words(a, c * CHUNK, CHUNK),
                        rhs_scale=word_plane[:, a, cols],
                        start=(a == 0),
                        stop=False,
                    )
                nc.tensor.matmul_mx(
                    out=bank[:],
                    lhsT=up_codes[half][:, within : within + P].bitcast(FP8X4),
                    lhsT_scale=up_plane[half][:, within : within + P],
                    rhs=h_codes[c][:].bitcast(FP8X4),
                    rhs_scale=h_plane[c][:],
                    start=False,
                    stop=True,
                )
                nc.scalar.activation(
                    activated[:, c * CHUNK - first : (c + 1) * CHUNK - first], bank[:], ACT.Silu, bias=bias[:, n : n + 1]
                )
            nc.vector.tensor_tensor(
                result[:, first : first + count],
                residual[n][:].indirect(picks(first, count)),
                activated[:],
                ADD,
            )

        def store(result, n, first, count):
            nc.sync.dma_start(out[n * P : (n + 1) * P, first : first + count], result[:, first : first + count])

        last = ROW_TILES - 1
        for n in range(last):
            result = outs.tile([P, S], F32, name=f"result{n}", tag="result")
            for first in range(0, S, PIECE):
                output_piece(result, n, first, PIECE)
            store(result, n, 0, S)
        result = outs.tile([P, S], F32, name=f"result{last}", tag="result")
        for first, count in ((0, PIECE), (PIECE, CHUNK), (PIECE + CHUNK, CHUNK)):
            output_piece(result, last, first, count)
            store(result, last, first, count)
